import numpy as np
import ml_dtypes


def mxq(x, axis, fmt="e4m3"):
    dtype, down = {"e4m3": (ml_dtypes.float8_e4m3fn, 7), "e5m2": (ml_dtypes.float8_e5m2, 14)}[fmt]
    v = np.moveaxis(np.asarray(x, np.float32).astype(ml_dtypes.bfloat16).astype(np.float64), axis, -1)
    blocks = v.reshape(v.shape[:-1] + (-1, 32))
    amax = np.abs(blocks).max(-1, keepdims=True)
    byte = np.maximum(np.where(amax > 0, np.frexp(amax)[1] - 1 + 127, 0) - down, 1)
    scale = np.exp2(byte - 127.0)
    codes = (blocks / scale).astype(np.float32).astype(dtype).astype(np.float64)
    return np.moveaxis((codes * scale).reshape(v.shape), -1, axis)


WIDE = False


def mx_kscale(k):
    if not WIDE:
        return np.ones(k)
    levels = np.array([10, -10, 5, -5, 0])
    if k % 512:
        return np.exp2(np.random.permutation(np.resize(levels, k // 32))).repeat(32)
    a = np.empty((k // 512, 16))
    for p in range(k // 512):
        a[p, :8] = np.random.permutation(np.resize(levels, 8))
        for g in range(8):
            far = levels[np.abs(levels - a[p, g]) >= 10]
            a[p, g + 8] = far[np.random.randint(len(far))]
    return np.exp2(a.ravel()).repeat(32)


def f64(x):
    return np.asarray(x).astype(np.float64)


def striped8(idx):
    return np.asarray(idx).reshape(8, -1, 16).transpose(0, 2, 1).reshape(128, -1).astype(np.uint16)


def unstriped8(offs):
    return offs.reshape(8, 16, -1).transpose(0, 2, 1).reshape(8, -1).astype(np.int64)


def pick8(x, idx, run):
    r = np.arange(len(x))
    return x[r[:, None], idx[r % (8 * run) // run]]


E2M1 = np.array([0.0, 0.5, 1.0, 1.5, 2.0, 3.0, 4.0, 6.0, -0.0, -0.5, -1.0, -1.5, -2.0, -3.0, -4.0, -6.0])


def pack_weight(w, fmt):
    k, n = w.shape
    w = f64(np.asarray(w, np.float32).astype(ml_dtypes.bfloat16)).reshape(k // 32, 32, n)
    amax = np.abs(w).max(1)
    if fmt == "e4m3":
        byte = np.frexp(amax)[1] - 1 + 127 - 7
    else:
        mant, ex = np.frexp(amax / 6.0)
        byte = np.where(mant > 0.5, ex, ex - 1) + 127
    byte = np.clip(np.where(amax > 0, byte, 1), 1, 254)
    scaled = (w * np.exp2(127.0 - byte)[:, None, :]).reshape(k, n).astype(np.float32)
    by_word = np.ascontiguousarray(scaled.reshape(k // 512, 128, 4, n).transpose(0, 1, 3, 2))
    if fmt == "e4m3":
        words = by_word.astype(ml_dtypes.float8_e4m3fn).view(np.uint8)
    else:
        c = by_word.astype(ml_dtypes.float4_e2m1fn).view(np.uint8) & 0xF
        words = (c[..., 0::2] | (c[..., 1::2] << 4)).reshape(k // 512, 128, 2 * n)
    return np.ascontiguousarray(words), np.ascontiguousarray(byte.astype(np.uint8).reshape(k // 512, 16, n))


def unpack_weight(words, scales, fmt):
    g, _, n = scales.shape
    words = np.ascontiguousarray(words).reshape(g, 128, n, -1)
    if fmt == "e4m3":
        vals = words.view(ml_dtypes.float8_e4m3fn).astype(np.float64)
    else:
        nib = np.empty((g, 128, n, 4), np.uint8)
        nib[..., 0::2] = words & 0xF
        nib[..., 1::2] = words >> 4
        vals = E2M1[nib]
    vals = vals * np.repeat(np.exp2(scales.astype(np.float64) - 127.0), 8, axis=1)[..., None]
    return vals.transpose(0, 1, 3, 2).reshape(g * 512, n)


D, V, Q, I = 512, 2048, 128, 512


def setup_inputs():
    n = np.random.standard_normal
    idx = np.stack([np.random.permutation(V)[:I] for _ in range(8)])
    fd = mx_kscale(D)
    vocp = pack_weight(n((D, V)) / fd[:, None], "e4m3")
    return {
        "hid": (n((D, Q)) * 1.0 / np.sqrt(D) * fd[:, None]).astype(np.float32),
        "voc_words": vocp[0],
        "voc_scales": vocp[1],
        "fac": (np.random.uniform(300.0, 1500.0, (Q, 1))).astype(np.float32),
        "sw": (np.random.uniform(0.5, 2.0, (1, I))).astype(np.float32),
        "old": (0.5 * n((Q, V))).astype(np.float32),
        "offs": striped8(idx),
    }


def reference(hid, voc_words, voc_scales, fac, sw, old, offs):
    idx = unstriped8(offs)
    vocu = unpack_weight(voc_words, voc_scales, "e4m3")
    hidq = mxq(f64(hid), 0, "e4m3")
    a = hidq.T @ vocu
    m1 = np.max(a, axis=1, keepdims=True)
    p = np.exp(a - m1)
    z = np.sum(p, axis=1, keepdims=True)
    px = np.exp(pick8(a, idx, 16) - m1)
    u1 = px / z * f64(fac) + 1.0
    du1 = f64(sw) * (-1.0) / u1
    dpx = du1 * f64(fac) / z
    dz = np.sum(du1 * f64(fac) * px / np.square(z) * (-1.0), axis=1, keepdims=True)
    e1 = dpx * px
    s1 = np.zeros((Q, V))
    s1[np.arange(Q)[:, None], idx[np.arange(Q) % 128 // 16]] = e1
    da = dz * p + s1
    y = da * 64.0 + f64(old)
    return y

@@ -1,0 +1,233 @@
+from contextlib import ExitStack
+
+import concourse.mybir as mybir
+from concourse.masks import make_identity
+
+D, V, Q, I = 512, 2048, 128, 512
+FLOPS = 2 * D * V * Q
+
+F32 = mybir.dt.float32
+BF16 = mybir.dt.bfloat16
+U32 = mybir.dt.uint32
+I32 = mybir.dt.int32
+U16 = mybir.dt.uint16
+U8 = mybir.dt.uint8
+FP8X4 = mybir.dt.float8_e4m3fn_x4
+ALU = mybir.AluOpType
+ACT = mybir.ActivationFunctionType
+
+P = 128
+BANK = 512
+GROUPS = V // BANK
+SHRINK = 2.0 ** -24
+CHUNKS = [(0, 256), (256, 256), (512, 512), (1024, 512), (1536, 512)]
+TURNED = [1, 2, 3]
+
+
+def tile_attend_bdiscouraged_heads_kernel(tc, hid, voc_words, voc_scales, fac, sw, old, offs, out):
+    nc = tc.nc
+    n_chunks = len(CHUNKS)
+    with ExitStack() as ctx:
+        sb = ctx.enter_context(tc.tile_pool(name="sb", bufs=1))
+        ps = ctx.enter_context(tc.psum_pool(name="ps", bufs=1))
+
+        def bank(b, name):
+            return ps.tile([P, BANK], F32, tag="bank%d" % b, name=name)
+
+        hid_raw = sb.tile([P, 4, Q], F32, name="hid_raw")
+        nc.sync.dma_start(out=hid_raw[:], in_=hid.rearrange("(p t) q -> p t q", t=4))
+
+        planes = sb.tile([P, BANK], U8, name="planes", align_bytes=64)
+        nc.vector.memset(planes[:].bitcast(I32), 0)
+        warm = sb.tile([P, 1], F32, name="warm")
+        nc.vector.memset(warm[:], 0.0)
+        scale_words = voc_scales[0].bitcast(I32)
+        for quad in range(4):
+            nc.scalar.dma_start(
+                out=planes[32 * quad : 32 * quad + 16, :].bitcast(I32),
+                in_=scale_words[4 * quad : 4 * quad + 4, :].rearrange("r (g c) -> g r c", g=GROUPS),
+            )
+        warm_out = sb.tile([P, 1], F32, name="warm_out")
+        nc.scalar.activation(out=warm_out[:], in_=warm[:], func=ACT.Exp)
+
+        word_rows = voc_words[0].rearrange("p n t -> p (n t)").bitcast(I32)
+        words = []
+        for g in range(GROUPS):
+            w = sb.tile([P, BANK], U32, name="words%d" % g, align_bytes=64)
+            nc.sync.dma_start(out=w[:].bitcast(I32), in_=word_rows[:, g * BANK : (g + 1) * BANK])
+            words.append(w)
+
+        offsets = sb.tile([P, I // 16], U16, name="offsets")
+        nc.sync.dma_start(offsets[:], offs)
+        fac_col = sb.tile([P, 1], F32, name="fac_col")
+        nc.sync.dma_start(out=fac_col[:], in_=fac)
+        sw_rows = sb.tile([P, I], F32, name="sw_rows")
+        nc.sync.dma_start(out=sw_rows[:], in_=sw[0].partition_broadcast(P))
+        olds = []
+        for g in range(GROUPS):
+            o = sb.tile([P, BANK], F32, name="old%d" % g)
+            nc.sync.dma_start(out=o[:], in_=old[:, g * BANK : (g + 1) * BANK])
+            olds.append(o)
+
+        listed = sb.tile([P, V], F32, name="listed")
+        nc.vector.memset(listed[:], 0.0)
+        ident = sb.tile([P, P], F32, name="ident")
+        make_identity(nc, ident[:])
+        fac_small = sb.tile([P, 1], F32, name="fac_small")
+        nc.gpsimd.tensor_scalar(fac_small[:], fac_col[:], SHRINK, 0.0, ALU.mult, ALU.add)
+        fac64 = sb.tile([P, 1], F32, name="fac64")
+        nc.gpsimd.tensor_scalar(fac64[:], fac_col[:], -64.0 * SHRINK, 0.0, ALU.mult, ALU.add)
+
+        grouped = sb.tile([P, Q, 4], BF16, name="grouped", align_bytes=64)
+        nc.vector.tensor_copy(
+            out=grouped[:].rearrange("p (c i) t -> p c t i", i=4),
+            in_=hid_raw[:].rearrange("p t (c i) -> p c t i", i=4),
+        )
+        hid_codes = sb.tile([P, Q], U32, name="hid_codes", align_bytes=64)
+        hid_scales = sb.tile([P, Q], U8, name="hid_scales", align_bytes=64)
+        nc.vector.quantize_mx(
+            out=hid_codes[:].bitcast(FP8X4), scales=hid_scales[:], in_=grouped[:].rearrange("p q t -> p (q t)")
+        )
+
+        a = sb.tile([P, V], F32, name="a")
+        p = sb.tile([P, V], F32, name="p")
+        run_max = sb.tile([P, n_chunks], F32, name="run_max")
+        neg_max = [sb.tile([P, 1], F32, name="neg_max%d" % j) for j in range(n_chunks)]
+        part_sum = sb.tile([P, n_chunks], F32, name="part_sum")
+        for j, (c0, n) in enumerate(CHUNKS):
+            g, off = divmod(c0, BANK)
+            acc = bank(j, "acc%d" % j)
+            nc.tensor.matmul_mx(
+                out=acc[:, 0:n],
+                lhsT=hid_codes[:].bitcast(FP8X4),
+                lhsT_scale=hid_scales[:],
+                rhs=words[g][:, off : off + n].bitcast(FP8X4),
+                rhs_scale=planes[4 * g : P, off : off + n],
+                start=True,
+                stop=True,
+            )
+            nc.vector.tensor_scalar(
+                a[:, c0 : c0 + n], acc[:, 0:n], 1.0, None, ALU.mult, ALU.max,
+                accum_out=run_max[:, j : j + 1],
+            )
+            if j < n_chunks - 1:
+                nc.gpsimd.tensor_scalar(neg_max[j][:], run_max[:, j : j + 1], -1.0, 0.0, ALU.mult, ALU.add)
+            else:
+                nc.vector.tensor_reduce(neg_max[j][:], run_max[:], mybir.AxisListType.X, ALU.max, negate=True)
+            nc.scalar.activation(
+                out=p[:, c0 : c0 + n], in_=a[:, c0 : c0 + n], func=ACT.Exp, bias=neg_max[j][:],
+                accum_out=part_sum[:, j : j + 1],
+            )
+        neg_m = neg_max[n_chunks - 1][:]
+
+        picked = sb.tile([P, I], F32, name="picked")
+        nc.vector.tensor_copy(picked[:], a[:].indirect(offsets[:]))
+
+        rescale = sb.tile([P, n_chunks], F32, name="rescale")
+        nc.vector.memset(rescale[:, n_chunks - 1 : n_chunks], 1.0)
+        nc.scalar.activation(
+            out=rescale[:, 0 : n_chunks - 1], in_=run_max[:, 0 : n_chunks - 1], func=ACT.Exp, bias=neg_m
+        )
+        px = sb.tile([P, I], F32, name="px")
+        half = I // 2
+        for h in range(2):
+            nc.scalar.activation(
+                out=px[:, h * half : (h + 1) * half], in_=picked[:, h * half : (h + 1) * half], func=ACT.Exp, bias=neg_m
+            )
+        terms = sb.tile([P, n_chunks], F32, name="terms")
+        z_small = sb.tile([P, 1], F32, name="z_small")
+        nc.vector.scalar_tensor_tensor(
+            terms[:], rescale[:], SHRINK, part_sum[:], ALU.mult, ALU.mult, accum_out=z_small[:]
+        )
+        z_inv = sb.tile([P, 1], F32, name="z_inv")
+        nc.vector.reciprocal(z_inv[:], z_small[:])
+        share = sb.tile([P, n_chunks], F32, name="share")
+        nc.vector.tensor_scalar(share[:], rescale[:], z_inv[:], -SHRINK, ALU.mult, ALU.mult)
+
+        sums_t = {}
+        for n, g in enumerate(TURNED):
+            sums_t[g] = bank(5 + n, "sum_t%d" % g)
+            for b in range(4):
+                nc.tensor.matmul(
+                    sums_t[g][:, b * P : (b + 1) * P], olds[g][:, b * P : (b + 1) * P], ident[:],
+                    start=(b == 0), stop=False, is_transpose=True,
+                )
+
+        den = sb.tile([P, I], F32, name="den")
+        for h in range(2):
+            nc.vector.tensor_scalar(
+                den[:, h * half : (h + 1) * half], px[:, h * half : (h + 1) * half], fac_small[:], z_small[:],
+                ALU.mult, ALU.add,
+            )
+        quarter = I // 4
+        pair = sb.tile([P, half], F32, name="pair")
+        nc.vector.tensor_tensor(pair[:], den[:, 0:half], den[:, half:I], ALU.mult)
+        four = sb.tile([P, quarter], F32, name="four")
+        nc.vector.tensor_tensor(four[:], pair[:, 0:quarter], pair[:, quarter:half], ALU.mult)
+        four_inv = sb.tile([P, quarter], F32, name="four_inv")
+        nc.vector.reciprocal(four_inv[:], four[:])
+        pair_inv = sb.tile([P, 2, quarter], F32, name="pair_inv")
+        nc.vector.tensor_tensor(
+            pair_inv[:],
+            four_inv[:].unsqueeze(1).to_broadcast([P, 2, quarter]),
+            pair[:].rearrange("p (s c) -> p s c", s=2)[:, ::-1, :],
+            ALU.mult,
+        )
+        weighted = sb.tile([P, I], F32, name="weighted")
+        crossed = sb.tile([P, I], F32, name="crossed")
+        for h in range(2):
+            mine = slice(h * half, (h + 1) * half)
+            nc.vector.scalar_tensor_tensor(weighted[:, mine], px[:, mine], fac64[:], sw_rows[:, mine], ALU.mult, ALU.mult)
+        for h in range(2):
+            mine = slice(h * half, (h + 1) * half)
+            other = slice((1 - h) * half, (2 - h) * half)
+            nc.vector.tensor_tensor(crossed[:, mine], weighted[:, mine], den[:, other], ALU.mult)
+        e64 = sb.tile([P, I], F32, name="e64")
+        e_sum = sb.tile([P, 1], F32, name="e_sum")
+        nc.vector.scalar_tensor_tensor(
+            e64[:].rearrange("p (s c) -> p s c", s=2),
+            pair_inv[:].rearrange("p s c -> p (s c)").unsqueeze(1).to_broadcast([P, 2, half]),
+            1.0,
+            crossed[:].rearrange("p (s c) -> p s c", s=2),
+            ALU.mult, ALU.mult,
+            accum_out=e_sum[:],
+        )
+        nc.vector.tensor_copy(listed[:].indirect(offsets[:]), e64[:])
+
+        coef = sb.tile([P, n_chunks], F32, name="coef")
+        nc.scalar.activation(out=coef[:], in_=share[:], func=ACT.Copy, scale=e_sum[:])
+
+        dense = {}
+        cps = {}
+        sts = {}
+        for g in TURNED:
+            j = g + 1
+            cps[g] = sb.tile([P, BANK], F32, name="cp%d" % g)
+            nc.scalar.activation(
+                out=cps[g][:], in_=p[:, g * BANK : (g + 1) * BANK], func=ACT.Copy, scale=coef[:, j : j + 1]
+            )
+        for g in TURNED:
+            for b in range(4):
+                nc.tensor.matmul(
+                    sums_t[g][:, b * P : (b + 1) * P], cps[g][:, b * P : (b + 1) * P], ident[:],
+                    start=False, stop=(b == 3), is_transpose=True,
+                )
+        for g in TURNED:
+            sts[g] = sb.tile([P, BANK], F32, name="st%d" % g)
+            nc.scalar.copy(out=sts[g][:], in_=sums_t[g][:])
+        for n, g in enumerate(TURNED):
+            dense[g] = bank(n, "dense%d" % g)
+            for b in range(4):
+                nc.tensor.transpose(dense[g][:, b * P : (b + 1) * P], sts[g][:, b * P : (b + 1) * P], ident[:])
+
+        own = sb.tile([P, BANK], F32, name="own")
+        for j in range(2):
+            c0, n = CHUNKS[j]
+            nc.vector.scalar_tensor_tensor(
+                own[:, c0 : c0 + n], p[:, c0 : c0 + n], coef[:, j : j + 1], olds[0][:, c0 : c0 + n], ALU.mult, ALU.add
+            )
+        dense[0] = own
+        for g in range(GROUPS):
+            res = sb.tile([P, BANK], F32, name="res%d" % g)
+            nc.vector.tensor_tensor(res[:], dense[g][:], listed[:, g * BANK : (g + 1) * BANK], ALU.add)
+            nc.sync.dma_start(out=out[:, g * BANK : (g + 1) * BANK], in_=res[:])

@@ -19,9 +19,9 @@ ACT = mybir.ActivationFunctionType
 P = 128
 BANK = 512
 GROUPS = V // BANK
-SHRINK = 2.0 ** -24
+SHRINK = 2.0 ** -64
 CHUNKS = [(0, 256), (256, 256), (512, 512), (1024, 512), (1536, 512)]
-TURNED = [1, 2, 3]
+TURNED = [0, 1, 2]
 
 
 def tile_attend_bdiscouraged_heads_kernel(tc, hid, voc_words, voc_scales, fac, sw, old, offs, out):
@@ -42,23 +42,26 @@ def tile_attend_bdiscouraged_heads_kernel(tc, hid, voc_words, voc_scales, fac, s
         warm = sb.tile([P, 1], F32, name="warm")
         nc.vector.memset(warm[:], 0.0)
         scale_words = voc_scales[0].bitcast(I32)
-        for quad in range(4):
-            nc.scalar.dma_start(
-                out=planes[32 * quad : 32 * quad + 16, :].bitcast(I32),
-                in_=scale_words[4 * quad : 4 * quad + 4, :].rearrange("r (g c) -> g r c", g=GROUPS),
-            )
         warm_out = sb.tile([P, 1], F32, name="warm_out")
         nc.scalar.activation(out=warm_out[:], in_=warm[:], func=ACT.Exp)
 
         word_rows = voc_words[0].rearrange("p n t -> p (n t)").bitcast(I32)
-        words = []
-        for g in range(GROUPS):
-            w = sb.tile([P, BANK], U32, name="words%d" % g, align_bytes=64)
-            nc.sync.dma_start(out=w[:].bitcast(I32), in_=word_rows[:, g * BANK : (g + 1) * BANK])
-            words.append(w)
+        words = [sb.tile([P, BANK], U32, name="words%d" % g, align_bytes=64) for g in range(GROUPS)]
 
+        def load_words(g):
+            nc.sync.dma_start(out=words[g][:].bitcast(I32), in_=word_rows[:, g * BANK : (g + 1) * BANK])
+
+        load_words(0)
+        load_words(1)
         offsets = sb.tile([P, I // 16], U16, name="offsets")
         nc.sync.dma_start(offsets[:], offs)
+        for quad in range(4):
+            nc.sync.dma_start(
+                out=planes[32 * quad : 32 * quad + 16, :].bitcast(I32),
+                in_=scale_words[4 * quad : 4 * quad + 4, :].rearrange("r (g c) -> g r c", g=GROUPS),
+            )
+        load_words(2)
+        load_words(3)
         fac_col = sb.tile([P, 1], F32, name="fac_col")
         nc.sync.dma_start(out=fac_col[:], in_=fac)
         sw_rows = sb.tile([P, I], F32, name="sw_rows")
@@ -73,15 +76,15 @@ def tile_attend_bdiscouraged_heads_kernel(tc, hid, voc_words, voc_scales, fac, s
         nc.vector.memset(listed[:], 0.0)
         ident = sb.tile([P, P], F32, name="ident")
         make_identity(nc, ident[:])
-        fac_small = sb.tile([P, 1], F32, name="fac_small")
-        nc.gpsimd.tensor_scalar(fac_small[:], fac_col[:], SHRINK, 0.0, ALU.mult, ALU.add)
-        fac64 = sb.tile([P, 1], F32, name="fac64")
-        nc.gpsimd.tensor_scalar(fac64[:], fac_col[:], -64.0 * SHRINK, 0.0, ALU.mult, ALU.add)
 
         grouped = sb.tile([P, Q, 4], BF16, name="grouped", align_bytes=64)
         nc.vector.tensor_copy(
-            out=grouped[:].rearrange("p (c i) t -> p c t i", i=4),
-            in_=hid_raw[:].rearrange("p t (c i) -> p c t i", i=4),
+            out=grouped[:, 0:80, :].rearrange("p (c i) t -> p c t i", i=4),
+            in_=hid_raw[:, :, 0:80].rearrange("p t (c i) -> p c t i", i=4),
+        )
+        nc.scalar.copy(
+            out=grouped[:, 80:Q, :].rearrange("p (c i) t -> p c t i", i=4),
+            in_=hid_raw[:, :, 80:Q].rearrange("p t (c i) -> p c t i", i=4),
         )
         hid_codes = sb.tile([P, Q], U32, name="hid_codes", align_bytes=64)
         hid_scales = sb.tile([P, Q], U8, name="hid_scales", align_bytes=64)
@@ -92,8 +95,8 @@ def tile_attend_bdiscouraged_heads_kernel(tc, hid, voc_words, voc_scales, fac, s
         a = sb.tile([P, V], F32, name="a")
         p = sb.tile([P, V], F32, name="p")
         run_max = sb.tile([P, n_chunks], F32, name="run_max")
-        neg_max = [sb.tile([P, 1], F32, name="neg_max%d" % j) for j in range(n_chunks)]
-        part_sum = sb.tile([P, n_chunks], F32, name="part_sum")
+        neg_max = sb.tile([P, GROUPS], F32, name="neg_max")
+        part_sum = sb.tile([P, GROUPS], F32, name="part_sum")
         for j, (c0, n) in enumerate(CHUNKS):
             g, off = divmod(c0, BANK)
             acc = bank(j, "acc%d" % j)
@@ -110,39 +113,44 @@ def tile_attend_bdiscouraged_heads_kernel(tc, hid, voc_words, voc_scales, fac, s
                 a[:, c0 : c0 + n], acc[:, 0:n], 1.0, None, ALU.mult, ALU.max,
                 accum_out=run_max[:, j : j + 1],
             )
-            if j < n_chunks - 1:
-                nc.gpsimd.tensor_scalar(neg_max[j][:], run_max[:, j : j + 1], -1.0, 0.0, ALU.mult, ALU.add)
-            else:
-                nc.vector.tensor_reduce(neg_max[j][:], run_max[:], mybir.AxisListType.X, ALU.max, negate=True)
-            nc.scalar.activation(
-                out=p[:, c0 : c0 + n], in_=a[:, c0 : c0 + n], func=ACT.Exp, bias=neg_max[j][:],
-                accum_out=part_sum[:, j : j + 1],
+            if off + n < BANK:
+                continue
+            first = 0 if g in (0, GROUPS - 1) else j
+            nc.vector.tensor_reduce(
+                neg_max[:, g : g + 1], run_max[:, first : j + 1], mybir.AxisListType.X, ALU.max, negate=True
             )
-        neg_m = neg_max[n_chunks - 1][:]
+            cols = slice(g * BANK, (g + 1) * BANK)
+            nc.scalar.activation(
+                out=p[:, cols], in_=a[:, cols], func=ACT.Exp, bias=neg_max[:, g : g + 1],
+                accum_out=part_sum[:, g : g + 1],
+            )
+        neg_m = neg_max[:, GROUPS - 1 : GROUPS]
 
         picked = sb.tile([P, I], F32, name="picked")
         nc.vector.tensor_copy(picked[:], a[:].indirect(offsets[:]))
 
-        rescale = sb.tile([P, n_chunks], F32, name="rescale")
-        nc.vector.memset(rescale[:, n_chunks - 1 : n_chunks], 1.0)
-        nc.scalar.activation(
-            out=rescale[:, 0 : n_chunks - 1], in_=run_max[:, 0 : n_chunks - 1], func=ACT.Exp, bias=neg_m
-        )
+        rescale = sb.tile([P, GROUPS], F32, name="rescale")
+        nc.scalar.activation(out=rescale[:], in_=neg_max[:], func=ACT.Exp, scale=-1.0, bias=neg_m)
         px = sb.tile([P, I], F32, name="px")
         half = I // 2
         for h in range(2):
             nc.scalar.activation(
                 out=px[:, h * half : (h + 1) * half], in_=picked[:, h * half : (h + 1) * half], func=ACT.Exp, bias=neg_m
             )
-        terms = sb.tile([P, n_chunks], F32, name="terms")
+        terms = sb.tile([P, GROUPS], F32, name="terms")
         z_small = sb.tile([P, 1], F32, name="z_small")
         nc.vector.scalar_tensor_tensor(
-            terms[:], rescale[:], SHRINK, part_sum[:], ALU.mult, ALU.mult, accum_out=z_small[:]
+            terms[:], rescale[:], 1.0, part_sum[:], ALU.mult, ALU.mult, accum_out=z_small[:]
         )
         z_inv = sb.tile([P, 1], F32, name="z_inv")
         nc.vector.reciprocal(z_inv[:], z_small[:])
-        share = sb.tile([P, n_chunks], F32, name="share")
-        nc.vector.tensor_scalar(share[:], rescale[:], z_inv[:], -SHRINK, ALU.mult, ALU.mult)
+        share = sb.tile([P, GROUPS], F32, name="share")
+        nc.vector.tensor_scalar(share[:], rescale[:], z_inv[:], -1.0, ALU.mult, ALU.mult)
+
+        soft = sb.tile([P, V], F32, name="soft")
+        for g in range(GROUPS):
+            cols = slice(g * BANK, (g + 1) * BANK)
+            nc.scalar.activation(out=soft[:, cols], in_=p[:, cols], func=ACT.Copy, scale=share[:, g : g + 1])
 
         sums_t = {}
         for n, g in enumerate(TURNED):
@@ -156,28 +164,30 @@ def tile_attend_bdiscouraged_heads_kernel(tc, hid, voc_words, voc_scales, fac, s
         den = sb.tile([P, I], F32, name="den")
         for h in range(2):
             nc.vector.tensor_scalar(
-                den[:, h * half : (h + 1) * half], px[:, h * half : (h + 1) * half], fac_small[:], z_small[:],
+                den[:, h * half : (h + 1) * half], px[:, h * half : (h + 1) * half], fac_col[:], z_small[:],
                 ALU.mult, ALU.add,
             )
         quarter = I // 4
         pair = sb.tile([P, half], F32, name="pair")
         nc.vector.tensor_tensor(pair[:], den[:, 0:half], den[:, half:I], ALU.mult)
         four = sb.tile([P, quarter], F32, name="four")
-        nc.vector.tensor_tensor(four[:], pair[:, 0:quarter], pair[:, quarter:half], ALU.mult)
+        nc.vector.scalar_tensor_tensor(four[:], pair[:, 0:quarter], SHRINK, pair[:, quarter:half], ALU.mult, ALU.mult)
         four_inv = sb.tile([P, quarter], F32, name="four_inv")
         nc.vector.reciprocal(four_inv[:], four[:])
         pair_inv = sb.tile([P, 2, quarter], F32, name="pair_inv")
-        nc.vector.tensor_tensor(
+        nc.vector.scalar_tensor_tensor(
             pair_inv[:],
-            four_inv[:].unsqueeze(1).to_broadcast([P, 2, quarter]),
             pair[:].rearrange("p (s c) -> p s c", s=2)[:, ::-1, :],
+            SHRINK,
+            four_inv[:].unsqueeze(1).to_broadcast([P, 2, quarter]),
+            ALU.mult,
             ALU.mult,
         )
         weighted = sb.tile([P, I], F32, name="weighted")
         crossed = sb.tile([P, I], F32, name="crossed")
         for h in range(2):
             mine = slice(h * half, (h + 1) * half)
-            nc.vector.scalar_tensor_tensor(weighted[:, mine], px[:, mine], fac64[:], sw_rows[:, mine], ALU.mult, ALU.mult)
+            nc.vector.scalar_tensor_tensor(weighted[:, mine], px[:, mine], fac_col[:], sw_rows[:, mine], ALU.mult, ALU.mult)
         for h in range(2):
             mine = slice(h * half, (h + 1) * half)
             other = slice((1 - h) * half, (2 - h) * half)
@@ -187,47 +197,49 @@ def tile_attend_bdiscouraged_heads_kernel(tc, hid, voc_words, voc_scales, fac, s
         nc.vector.scalar_tensor_tensor(
             e64[:].rearrange("p (s c) -> p s c", s=2),
             pair_inv[:].rearrange("p s c -> p (s c)").unsqueeze(1).to_broadcast([P, 2, half]),
-            1.0,
+            -64.0,
             crossed[:].rearrange("p (s c) -> p s c", s=2),
             ALU.mult, ALU.mult,
             accum_out=e_sum[:],
         )
         nc.vector.tensor_copy(listed[:].indirect(offsets[:]), e64[:])
 
-        coef = sb.tile([P, n_chunks], F32, name="coef")
-        nc.scalar.activation(out=coef[:], in_=share[:], func=ACT.Copy, scale=e_sum[:])
 
         dense = {}
         cps = {}
         sts = {}
-        for g in TURNED:
-            j = g + 1
+
+        def scale_and_add(g):
             cps[g] = sb.tile([P, BANK], F32, name="cp%d" % g)
-            nc.scalar.activation(
-                out=cps[g][:], in_=p[:, g * BANK : (g + 1) * BANK], func=ACT.Copy, scale=coef[:, j : j + 1]
-            )
-        for g in TURNED:
+            nc.scalar.activation(out=cps[g][:], in_=soft[:, g * BANK : (g + 1) * BANK], func=ACT.Copy, scale=e_sum[:])
             for b in range(4):
                 nc.tensor.matmul(
                     sums_t[g][:, b * P : (b + 1) * P], cps[g][:, b * P : (b + 1) * P], ident[:],
                     start=False, stop=(b == 3), is_transpose=True,
                 )
-        for g in TURNED:
+
+        def empty(g):
             sts[g] = sb.tile([P, BANK], F32, name="st%d" % g)
             nc.scalar.copy(out=sts[g][:], in_=sums_t[g][:])
+
+        for g in TURNED:
+            scale_and_add(g)
+        for g in TURNED:
+            empty(g)
         for n, g in enumerate(TURNED):
             dense[g] = bank(n, "dense%d" % g)
             for b in range(4):
                 nc.tensor.transpose(dense[g][:, b * P : (b + 1) * P], sts[g][:, b * P : (b + 1) * P], ident[:])
 
+        own_cp = sb.tile([P, BANK], F32, name="own_cp")
+        nc.gpsimd.tensor_scalar(own_cp[:], soft[:, 3 * BANK : V], e_sum[:], 0.0, ALU.mult, ALU.add)
         own = sb.tile([P, BANK], F32, name="own")
-        for j in range(2):
-            c0, n = CHUNKS[j]
-            nc.vector.scalar_tensor_tensor(
-                own[:, c0 : c0 + n], p[:, c0 : c0 + n], coef[:, j : j + 1], olds[0][:, c0 : c0 + n], ALU.mult, ALU.add
-            )
-        dense[0] = own
-        for g in range(GROUPS):
-            res = sb.tile([P, BANK], F32, name="res%d" % g)
-            nc.vector.tensor_tensor(res[:], dense[g][:], listed[:, g * BANK : (g + 1) * BANK], ALU.add)
-            nc.sync.dma_start(out=out[:, g * BANK : (g + 1) * BANK], in_=res[:])
+        nc.gpsimd.tensor_tensor(own[:], own_cp[:], olds[3][:], ALU.add)
+        for g, lo, hi in [(0, 0, 256), (0, 256, 512), (1, 0, 512), (3, 0, 512), (2, 0, 256), (2, 256, 512)]:
+            res = sb.tile([P, hi - lo], F32, name="res%d_%d" % (g, lo)) if g in TURNED else sts[0]
+            cols = slice(g * BANK + lo, g * BANK + hi)
+            if g in TURNED:
+                nc.vector.tensor_tensor(res[:], dense[g][:, lo:hi], listed[:, cols], ALU.add)
+            else:
+                nc.gpsimd.tensor_tensor(res[:], own[:, lo:hi], listed[:, cols], ALU.add)
+            nc.sync.dma_start(out=out[:, cols], in_=res[:])

@@ -21,7 +21,8 @@ BANK = 512
 GROUPS = V // BANK
 SHRINK = 2.0 ** -64
 CHUNKS = [(0, 256), (256, 256), (512, 512), (1024, 512), (1536, 512)]
-TURNED = [0, 1, 2]
+TURNED = [(0, 256), (256, 512), (768, 512)]
+POOLED = [(1280, 256), (1536, 512)]
 
 
 def tile_attend_bdiscouraged_heads_kernel(tc, hid, voc_words, voc_scales, fac, sw, old, offs, out):
@@ -52,7 +53,6 @@ def tile_attend_bdiscouraged_heads_kernel(tc, hid, voc_words, voc_scales, fac, s
             nc.sync.dma_start(out=words[g][:].bitcast(I32), in_=word_rows[:, g * BANK : (g + 1) * BANK])
 
         load_words(0)
-        load_words(1)
         offsets = sb.tile([P, I // 16], U16, name="offsets")
         nc.sync.dma_start(offsets[:], offs)
         for quad in range(4):
@@ -60,16 +60,18 @@ def tile_attend_bdiscouraged_heads_kernel(tc, hid, voc_words, voc_scales, fac, s
                 out=planes[32 * quad : 32 * quad + 16, :].bitcast(I32),
                 in_=scale_words[4 * quad : 4 * quad + 4, :].rearrange("r (g c) -> g r c", g=GROUPS),
             )
+        load_words(1)
         load_words(2)
         load_words(3)
         fac_col = sb.tile([P, 1], F32, name="fac_col")
         nc.sync.dma_start(out=fac_col[:], in_=fac)
         sw_rows = sb.tile([P, I], F32, name="sw_rows")
         nc.sync.dma_start(out=sw_rows[:], in_=sw[0].partition_broadcast(P))
+        pooled0 = POOLED[0][0]
         olds = []
-        for g in range(GROUPS):
-            o = sb.tile([P, BANK], F32, name="old%d" % g)
-            nc.sync.dma_start(out=o[:], in_=old[:, g * BANK : (g + 1) * BANK])
+        for u, (c0, n) in enumerate(TURNED + [(pooled0, V - pooled0)]):
+            o = sb.tile([P, n], F32, name="old%d" % u)
+            nc.sync.dma_start(out=o[:], in_=old[:, c0 : c0 + n])
             olds.append(o)
 
         listed = sb.tile([P, V], F32, name="listed")
@@ -79,12 +81,8 @@ def tile_attend_bdiscouraged_heads_kernel(tc, hid, voc_words, voc_scales, fac, s
 
         grouped = sb.tile([P, Q, 4], BF16, name="grouped", align_bytes=64)
         nc.vector.tensor_copy(
-            out=grouped[:, 0:80, :].rearrange("p (c i) t -> p c t i", i=4),
-            in_=hid_raw[:, :, 0:80].rearrange("p t (c i) -> p c t i", i=4),
-        )
-        nc.scalar.copy(
-            out=grouped[:, 80:Q, :].rearrange("p (c i) t -> p c t i", i=4),
-            in_=hid_raw[:, :, 80:Q].rearrange("p t (c i) -> p c t i", i=4),
+            out=grouped[:].rearrange("p (c i) t -> p c t i", i=4),
+            in_=hid_raw[:].rearrange("p t (c i) -> p c t i", i=4),
         )
         hid_codes = sb.tile([P, Q], U32, name="hid_codes", align_bytes=64)
         hid_scales = sb.tile([P, Q], U8, name="hid_scales", align_bytes=64)
@@ -140,24 +138,24 @@ def tile_attend_bdiscouraged_heads_kernel(tc, hid, voc_words, voc_scales, fac, s
         terms = sb.tile([P, GROUPS], F32, name="terms")
         z_small = sb.tile([P, 1], F32, name="z_small")
         nc.vector.scalar_tensor_tensor(
-            terms[:], rescale[:], 1.0, part_sum[:], ALU.mult, ALU.mult, accum_out=z_small[:]
+            terms[:], rescale[:], -1.0, part_sum[:], ALU.mult, ALU.mult, accum_out=z_small[:]
         )
         z_inv = sb.tile([P, 1], F32, name="z_inv")
         nc.vector.reciprocal(z_inv[:], z_small[:])
         share = sb.tile([P, GROUPS], F32, name="share")
-        nc.vector.tensor_scalar(share[:], rescale[:], z_inv[:], -1.0, ALU.mult, ALU.mult)
+        nc.scalar.activation(out=share[:], in_=rescale[:], func=ACT.Copy, scale=z_inv[:])
 
         soft = sb.tile([P, V], F32, name="soft")
         for g in range(GROUPS):
             cols = slice(g * BANK, (g + 1) * BANK)
             nc.scalar.activation(out=soft[:, cols], in_=p[:, cols], func=ACT.Copy, scale=share[:, g : g + 1])
 
-        sums_t = {}
-        for n, g in enumerate(TURNED):
-            sums_t[g] = bank(5 + n, "sum_t%d" % g)
-            for b in range(4):
+        sums_t = []
+        for u, (c0, n) in enumerate(TURNED):
+            sums_t.append(bank(5 + u, "sum_t%d" % u))
+            for b in range(n // P):
                 nc.tensor.matmul(
-                    sums_t[g][:, b * P : (b + 1) * P], olds[g][:, b * P : (b + 1) * P], ident[:],
+                    sums_t[u][:, b * P : (b + 1) * P], olds[u][:, b * P : (b + 1) * P], ident[:],
                     start=(b == 0), stop=False, is_transpose=True,
                 )
 
@@ -165,7 +163,7 @@ def tile_attend_bdiscouraged_heads_kernel(tc, hid, voc_words, voc_scales, fac, s
         for h in range(2):
             nc.vector.tensor_scalar(
                 den[:, h * half : (h + 1) * half], px[:, h * half : (h + 1) * half], fac_col[:], z_small[:],
-                ALU.mult, ALU.add,
+                ALU.mult, ALU.subtract,
             )
         quarter = I // 4
         pair = sb.tile([P, half], F32, name="pair")
@@ -205,41 +203,43 @@ def tile_attend_bdiscouraged_heads_kernel(tc, hid, voc_words, voc_scales, fac, s
         nc.vector.tensor_copy(listed[:].indirect(offsets[:]), e64[:])
 
 
-        dense = {}
-        cps = {}
-        sts = {}
-
-        def scale_and_add(g):
-            cps[g] = sb.tile([P, BANK], F32, name="cp%d" % g)
-            nc.scalar.activation(out=cps[g][:], in_=soft[:, g * BANK : (g + 1) * BANK], func=ACT.Copy, scale=e_sum[:])
-            for b in range(4):
+        for u, (c0, n) in enumerate(TURNED):
+            cp = sb.tile([P, n], F32, name="cp%d" % u)
+            nc.scalar.activation(out=cp[:], in_=soft[:, c0 : c0 + n], func=ACT.Copy, scale=e_sum[:])
+            for b in range(n // P):
                 nc.tensor.matmul(
-                    sums_t[g][:, b * P : (b + 1) * P], cps[g][:, b * P : (b + 1) * P], ident[:],
-                    start=False, stop=(b == 3), is_transpose=True,
+                    sums_t[u][:, b * P : (b + 1) * P], cp[:, b * P : (b + 1) * P], ident[:],
+                    start=False, stop=(b == n // P - 1), is_transpose=True,
                 )
+        sts = []
+        dense = []
+        for u, (c0, n) in enumerate(TURNED):
+            sts.append(sb.tile([P, n], F32, name="st%d" % u))
+            nc.scalar.copy(out=sts[u][:], in_=sums_t[u][:, 0:n])
+            dense.append(bank(u, "dense%d" % u))
+            for b in range(n // P):
+                nc.tensor.transpose(dense[u][:, b * P : (b + 1) * P], sts[u][:, b * P : (b + 1) * P], ident[:])
 
-        def empty(g):
-            sts[g] = sb.tile([P, BANK], F32, name="st%d" % g)
-            nc.scalar.copy(out=sts[g][:], in_=sums_t[g][:])
+        own_cp = sb.tile([P, V - pooled0], F32, name="own_cp")
+        nc.gpsimd.tensor_scalar(own_cp[:], soft[:, pooled0:V], e_sum[:], 0.0, ALU.mult, ALU.add)
+        room = sb.tile([P, 1024], F32, name="room")
+        own = room[:, 256:1024]
+        nc.gpsimd.tensor_tensor(own, own_cp[:], olds[len(TURNED)][:], ALU.add)
 
-        for g in TURNED:
-            scale_and_add(g)
-        for g in TURNED:
-            empty(g)
-        for n, g in enumerate(TURNED):
-            dense[g] = bank(n, "dense%d" % g)
-            for b in range(4):
-                nc.tensor.transpose(dense[g][:, b * P : (b + 1) * P], sts[g][:, b * P : (b + 1) * P], ident[:])
+        def finish_turned(u, lo, hi):
+            c0 = TURNED[u][0]
+            res = sb.tile([P, hi - lo], F32, name="res%d_%d" % (u, lo))
+            nc.vector.tensor_tensor(res[:], dense[u][:, lo:hi], listed[:, c0 + lo : c0 + hi], ALU.add)
+            nc.sync.dma_start(out=out[:, c0 + lo : c0 + hi], in_=res[:])
 
-        own_cp = sb.tile([P, BANK], F32, name="own_cp")
-        nc.gpsimd.tensor_scalar(own_cp[:], soft[:, 3 * BANK : V], e_sum[:], 0.0, ALU.mult, ALU.add)
-        own = sb.tile([P, BANK], F32, name="own")
-        nc.gpsimd.tensor_tensor(own[:], own_cp[:], olds[3][:], ALU.add)
-        for g, lo, hi in [(0, 0, 256), (0, 256, 512), (1, 0, 512), (3, 0, 512), (2, 0, 256), (2, 256, 512)]:
-            res = sb.tile([P, hi - lo], F32, name="res%d_%d" % (g, lo)) if g in TURNED else sts[0]
-            cols = slice(g * BANK + lo, g * BANK + hi)
-            if g in TURNED:
-                nc.vector.tensor_tensor(res[:], dense[g][:, lo:hi], listed[:, cols], ALU.add)
-            else:
-                nc.gpsimd.tensor_tensor(res[:], own[:, lo:hi], listed[:, cols], ALU.add)
-            nc.sync.dma_start(out=out[:, cols], in_=res[:])
+        c0, n = POOLED[0]
+        first = sb.tile([P, n], F32, name="first")
+        nc.vector.tensor_tensor(first[:], own[:, 0:n], listed[:, c0 : c0 + n], ALU.add)
+        nc.sync.dma_start(out=out[:, c0 : c0 + n], in_=first[:])
+        c0, n = POOLED[1]
+        nc.gpsimd.tensor_tensor(room[:, 0:n], own[:, c0 - pooled0 : V - pooled0], listed[:, c0:V], ALU.add)
+        nc.scalar.dma_start(out=out[:, c0:V], in_=room[:, 0:n])
+        finish_turned(0, 0, 256)
+        finish_turned(1, 0, 512)
+        finish_turned(2, 0, 256)
+        finish_turned(2, 256, 512)

@@ -17,34 +17,35 @@ ALU = mybir.AluOpType
 ACT = mybir.ActivationFunctionType
 
 P = 128
+PACK = 4
 BANK = 512
 GROUPS = V // BANK
-SHRINK = 2.0 ** -64
+HALF = I // 2
+QUARTER = I // 4
+
+SHRINK = 2.0**-64
+
 CHUNKS = [(0, 256), (256, 256), (512, 512), (1024, 512), (1536, 512)]
+
 TURNED = [(0, 256), (256, 512), (768, 512)]
-POOLED = [(1280, 256), (1536, 512)]
+EARLY = (1280, 256)
+LATE = (1536, 512)
 
 
 def tile_attend_bdiscouraged_heads_kernel(tc, hid, voc_words, voc_scales, fac, sw, old, offs, out):
     nc = tc.nc
-    n_chunks = len(CHUNKS)
     with ExitStack() as ctx:
         sb = ctx.enter_context(tc.tile_pool(name="sb", bufs=1))
         ps = ctx.enter_context(tc.psum_pool(name="ps", bufs=1))
 
-        def bank(b, name):
-            return ps.tile([P, BANK], F32, tag="bank%d" % b, name=name)
+        def bank(number, name):
+            return ps.tile([P, BANK], F32, tag="bank%d" % number, name=name)
 
-        hid_raw = sb.tile([P, 4, Q], F32, name="hid_raw")
-        nc.sync.dma_start(out=hid_raw[:], in_=hid.rearrange("(p t) q -> p t q", t=4))
+        hid_raw = sb.tile([P, PACK, Q], F32, name="hid_raw")
+        nc.sync.dma_start(out=hid_raw[:], in_=hid.rearrange("(p t) q -> p t q", t=PACK))
 
-        planes = sb.tile([P, BANK], U8, name="planes", align_bytes=64)
-        nc.vector.memset(planes[:].bitcast(I32), 0)
-        warm = sb.tile([P, 1], F32, name="warm")
-        nc.vector.memset(warm[:], 0.0)
-        scale_words = voc_scales[0].bitcast(I32)
-        warm_out = sb.tile([P, 1], F32, name="warm_out")
-        nc.scalar.activation(out=warm_out[:], in_=warm[:], func=ACT.Exp)
+        voc_planes = sb.tile([P, BANK], U8, name="voc_planes", align_bytes=64)
+        nc.vector.memset(voc_planes[:].bitcast(I32), 0)
 
         word_rows = voc_words[0].rearrange("p n t -> p (n t)").bitcast(I32)
         words = [sb.tile([P, BANK], U32, name="words%d" % g, align_bytes=64) for g in range(GROUPS)]
@@ -53,33 +54,34 @@ def tile_attend_bdiscouraged_heads_kernel(tc, hid, voc_words, voc_scales, fac, s
             nc.sync.dma_start(out=words[g][:].bitcast(I32), in_=word_rows[:, g * BANK : (g + 1) * BANK])
 
         load_words(0)
+        scale_rows = voc_scales[0].bitcast(I32)
+        for quadrant in range(4):
+            nc.sync.dma_start(
+                out=voc_planes[32 * quadrant : 32 * quadrant + 4 * GROUPS, :].bitcast(I32),
+                in_=scale_rows[4 * quadrant : 4 * quadrant + 4, :].rearrange("r (g c) -> g r c", g=GROUPS),
+            )
+        for g in range(1, GROUPS):
+            load_words(g)
         offsets = sb.tile([P, I // 16], U16, name="offsets")
         nc.sync.dma_start(offsets[:], offs)
-        for quad in range(4):
-            nc.sync.dma_start(
-                out=planes[32 * quad : 32 * quad + 16, :].bitcast(I32),
-                in_=scale_words[4 * quad : 4 * quad + 4, :].rearrange("r (g c) -> g r c", g=GROUPS),
-            )
-        load_words(1)
-        load_words(2)
-        load_words(3)
         fac_col = sb.tile([P, 1], F32, name="fac_col")
         nc.sync.dma_start(out=fac_col[:], in_=fac)
         sw_rows = sb.tile([P, I], F32, name="sw_rows")
         nc.sync.dma_start(out=sw_rows[:], in_=sw[0].partition_broadcast(P))
-        pooled0 = POOLED[0][0]
-        olds = []
-        for u, (c0, n) in enumerate(TURNED + [(pooled0, V - pooled0)]):
-            o = sb.tile([P, n], F32, name="old%d" % u)
-            nc.sync.dma_start(out=o[:], in_=old[:, c0 : c0 + n])
-            olds.append(o)
+        old_turned = []
+        for u, (c0, n) in enumerate(TURNED):
+            old_turned.append(sb.tile([P, n], F32, name="old_turned%d" % u))
+            nc.sync.dma_start(out=old_turned[u][:], in_=old[:, c0 : c0 + n])
+        pool0 = EARLY[0]
+        old_pool = sb.tile([P, V - pool0], F32, name="old_pool")
+        nc.sync.dma_start(out=old_pool[:], in_=old[:, pool0:V])
 
         listed = sb.tile([P, V], F32, name="listed")
         nc.vector.memset(listed[:], 0.0)
         ident = sb.tile([P, P], F32, name="ident")
         make_identity(nc, ident[:])
 
-        grouped = sb.tile([P, Q, 4], BF16, name="grouped", align_bytes=64)
+        grouped = sb.tile([P, Q, PACK], BF16, name="grouped", align_bytes=64)
         nc.vector.tensor_copy(
             out=grouped[:].rearrange("p (c i) t -> p c t i", i=4),
             in_=hid_raw[:].rearrange("p t (c i) -> p c t i", i=4),
@@ -91,155 +93,148 @@ def tile_attend_bdiscouraged_heads_kernel(tc, hid, voc_words, voc_scales, fac, s
         )
 
         a = sb.tile([P, V], F32, name="a")
-        p = sb.tile([P, V], F32, name="p")
-        run_max = sb.tile([P, n_chunks], F32, name="run_max")
-        neg_max = sb.tile([P, GROUPS], F32, name="neg_max")
-        part_sum = sb.tile([P, GROUPS], F32, name="part_sum")
+        p_group = sb.tile([P, V], F32, name="p_group")
+        chunk_max = sb.tile([P, len(CHUNKS)], F32, name="chunk_max")
+        neg_shift = sb.tile([P, GROUPS], F32, name="neg_shift")
+        group_sum = sb.tile([P, GROUPS], F32, name="group_sum")
         for j, (c0, n) in enumerate(CHUNKS):
             g, off = divmod(c0, BANK)
-            acc = bank(j, "acc%d" % j)
+            scores = bank(j, "scores%d" % j)
             nc.tensor.matmul_mx(
-                out=acc[:, 0:n],
+                out=scores[:, 0:n],
                 lhsT=hid_codes[:].bitcast(FP8X4),
                 lhsT_scale=hid_scales[:],
                 rhs=words[g][:, off : off + n].bitcast(FP8X4),
-                rhs_scale=planes[4 * g : P, off : off + n],
+                rhs_scale=voc_planes[4 * g : P, off : off + n],
                 start=True,
                 stop=True,
             )
             nc.vector.tensor_scalar(
-                a[:, c0 : c0 + n], acc[:, 0:n], 1.0, None, ALU.mult, ALU.max,
-                accum_out=run_max[:, j : j + 1],
+                a[:, c0 : c0 + n], scores[:, 0:n], 1.0, None, ALU.mult, ALU.max, accum_out=chunk_max[:, j : j + 1]
             )
             if off + n < BANK:
                 continue
-            first = 0 if g in (0, GROUPS - 1) else j
+            since = 0 if g in (0, GROUPS - 1) else j
             nc.vector.tensor_reduce(
-                neg_max[:, g : g + 1], run_max[:, first : j + 1], mybir.AxisListType.X, ALU.max, negate=True
+                neg_shift[:, g : g + 1], chunk_max[:, since : j + 1], mybir.AxisListType.X, ALU.max, negate=True
             )
             cols = slice(g * BANK, (g + 1) * BANK)
             nc.scalar.activation(
-                out=p[:, cols], in_=a[:, cols], func=ACT.Exp, bias=neg_max[:, g : g + 1],
-                accum_out=part_sum[:, g : g + 1],
+                out=p_group[:, cols],
+                in_=a[:, cols],
+                func=ACT.Exp,
+                bias=neg_shift[:, g : g + 1],
+                accum_out=group_sum[:, g : g + 1],
             )
-        neg_m = neg_max[:, GROUPS - 1 : GROUPS]
+        neg_max = neg_shift[:, GROUPS - 1 : GROUPS]
 
         picked = sb.tile([P, I], F32, name="picked")
         nc.vector.tensor_copy(picked[:], a[:].indirect(offsets[:]))
 
         rescale = sb.tile([P, GROUPS], F32, name="rescale")
-        nc.scalar.activation(out=rescale[:], in_=neg_max[:], func=ACT.Exp, scale=-1.0, bias=neg_m)
+        nc.scalar.activation(out=rescale[:], in_=neg_shift[:], func=ACT.Exp, scale=-1.0, bias=neg_max)
+        halves = [slice(0, HALF), slice(HALF, I)]
         px = sb.tile([P, I], F32, name="px")
-        half = I // 2
-        for h in range(2):
-            nc.scalar.activation(
-                out=px[:, h * half : (h + 1) * half], in_=picked[:, h * half : (h + 1) * half], func=ACT.Exp, bias=neg_m
-            )
-        terms = sb.tile([P, GROUPS], F32, name="terms")
-        z_small = sb.tile([P, 1], F32, name="z_small")
-        nc.vector.scalar_tensor_tensor(
-            terms[:], rescale[:], -1.0, part_sum[:], ALU.mult, ALU.mult, accum_out=z_small[:]
-        )
-        z_inv = sb.tile([P, 1], F32, name="z_inv")
-        nc.vector.reciprocal(z_inv[:], z_small[:])
-        share = sb.tile([P, GROUPS], F32, name="share")
-        nc.scalar.activation(out=share[:], in_=rescale[:], func=ACT.Copy, scale=z_inv[:])
+        for mine in halves:
+            nc.scalar.activation(out=px[:, mine], in_=picked[:, mine], func=ACT.Exp, bias=neg_max)
 
+        neg_terms = sb.tile([P, GROUPS], F32, name="neg_terms")
+        neg_z = sb.tile([P, 1], F32, name="neg_z")
+        nc.vector.scalar_tensor_tensor(
+            neg_terms[:], rescale[:], -1.0, group_sum[:], ALU.mult, ALU.mult, accum_out=neg_z[:]
+        )
+        neg_z_inv = sb.tile([P, 1], F32, name="neg_z_inv")
+        nc.vector.reciprocal(neg_z_inv[:], neg_z[:])
+        group_factor = sb.tile([P, GROUPS], F32, name="group_factor")
+        nc.scalar.activation(out=group_factor[:], in_=rescale[:], func=ACT.Copy, scale=neg_z_inv[:])
         soft = sb.tile([P, V], F32, name="soft")
         for g in range(GROUPS):
             cols = slice(g * BANK, (g + 1) * BANK)
-            nc.scalar.activation(out=soft[:, cols], in_=p[:, cols], func=ACT.Copy, scale=share[:, g : g + 1])
+            nc.scalar.activation(out=soft[:, cols], in_=p_group[:, cols], func=ACT.Copy, scale=group_factor[:, g : g + 1])
 
-        sums_t = []
+        sum_t = []
         for u, (c0, n) in enumerate(TURNED):
-            sums_t.append(bank(5 + u, "sum_t%d" % u))
+            sum_t.append(bank(len(CHUNKS) + u, "sum_t%d" % u))
             for b in range(n // P):
+                block = slice(b * P, (b + 1) * P)
                 nc.tensor.matmul(
-                    sums_t[u][:, b * P : (b + 1) * P], olds[u][:, b * P : (b + 1) * P], ident[:],
-                    start=(b == 0), stop=False, is_transpose=True,
+                    sum_t[u][:, block], old_turned[u][:, block], ident[:], start=(b == 0), stop=False, is_transpose=True
                 )
 
         den = sb.tile([P, I], F32, name="den")
-        for h in range(2):
-            nc.vector.tensor_scalar(
-                den[:, h * half : (h + 1) * half], px[:, h * half : (h + 1) * half], fac_col[:], z_small[:],
-                ALU.mult, ALU.subtract,
-            )
-        quarter = I // 4
-        pair = sb.tile([P, half], F32, name="pair")
-        nc.vector.tensor_tensor(pair[:], den[:, 0:half], den[:, half:I], ALU.mult)
-        four = sb.tile([P, quarter], F32, name="four")
-        nc.vector.scalar_tensor_tensor(four[:], pair[:, 0:quarter], SHRINK, pair[:, quarter:half], ALU.mult, ALU.mult)
-        four_inv = sb.tile([P, quarter], F32, name="four_inv")
+        for mine in halves:
+            nc.vector.tensor_scalar(den[:, mine], px[:, mine], fac_col[:], neg_z[:], ALU.mult, ALU.subtract)
+        pair = sb.tile([P, HALF], F32, name="pair")
+        nc.vector.tensor_tensor(pair[:], den[:, 0:HALF], den[:, HALF:I], ALU.mult)
+        four = sb.tile([P, QUARTER], F32, name="four")
+        nc.vector.scalar_tensor_tensor(four[:], pair[:, 0:QUARTER], SHRINK, pair[:, QUARTER:HALF], ALU.mult, ALU.mult)
+        four_inv = sb.tile([P, QUARTER], F32, name="four_inv")
         nc.vector.reciprocal(four_inv[:], four[:])
-        pair_inv = sb.tile([P, 2, quarter], F32, name="pair_inv")
+        pair_inv = sb.tile([P, 2, QUARTER], F32, name="pair_inv")
         nc.vector.scalar_tensor_tensor(
             pair_inv[:],
             pair[:].rearrange("p (s c) -> p s c", s=2)[:, ::-1, :],
             SHRINK,
-            four_inv[:].unsqueeze(1).to_broadcast([P, 2, quarter]),
+            four_inv[:].unsqueeze(1).to_broadcast([P, 2, QUARTER]),
             ALU.mult,
             ALU.mult,
         )
-        weighted = sb.tile([P, I], F32, name="weighted")
+        numer = sb.tile([P, I], F32, name="numer")
         crossed = sb.tile([P, I], F32, name="crossed")
-        for h in range(2):
-            mine = slice(h * half, (h + 1) * half)
-            nc.vector.scalar_tensor_tensor(weighted[:, mine], px[:, mine], fac_col[:], sw_rows[:, mine], ALU.mult, ALU.mult)
-        for h in range(2):
-            mine = slice(h * half, (h + 1) * half)
-            other = slice((1 - h) * half, (2 - h) * half)
-            nc.vector.tensor_tensor(crossed[:, mine], weighted[:, mine], den[:, other], ALU.mult)
+        for mine in halves:
+            nc.vector.scalar_tensor_tensor(numer[:, mine], px[:, mine], fac_col[:], sw_rows[:, mine], ALU.mult, ALU.mult)
+        for mine, partner in zip(halves, reversed(halves)):
+            nc.vector.tensor_tensor(crossed[:, mine], numer[:, mine], den[:, partner], ALU.mult)
         e64 = sb.tile([P, I], F32, name="e64")
-        e_sum = sb.tile([P, 1], F32, name="e_sum")
+        e64_sum = sb.tile([P, 1], F32, name="e64_sum")
         nc.vector.scalar_tensor_tensor(
             e64[:].rearrange("p (s c) -> p s c", s=2),
-            pair_inv[:].rearrange("p s c -> p (s c)").unsqueeze(1).to_broadcast([P, 2, half]),
+            pair_inv[:].rearrange("p s c -> p (s c)").unsqueeze(1).to_broadcast([P, 2, HALF]),
             -64.0,
             crossed[:].rearrange("p (s c) -> p s c", s=2),
-            ALU.mult, ALU.mult,
-            accum_out=e_sum[:],
+            ALU.mult,
+            ALU.mult,
+            accum_out=e64_sum[:],
         )
         nc.vector.tensor_copy(listed[:].indirect(offsets[:]), e64[:])
 
+        last = len(TURNED) - 1
+        scaled_width = TURNED[last][1]
+        shared = sb.tile([P, scaled_width + V - pool0], F32, name="shared")
+        dense_pool = shared[:, scaled_width : scaled_width + V - pool0]
+        late_done = shared[:, scaled_width + EARLY[1] - LATE[1] : scaled_width + EARLY[1]]
 
         for u, (c0, n) in enumerate(TURNED):
-            cp = sb.tile([P, n], F32, name="cp%d" % u)
-            nc.scalar.activation(out=cp[:], in_=soft[:, c0 : c0 + n], func=ACT.Copy, scale=e_sum[:])
+            scaled = shared[:, 0:n] if u == last else sb.tile([P, n], F32, name="scaled%d" % u)[:]
+            nc.scalar.activation(out=scaled, in_=soft[:, c0 : c0 + n], func=ACT.Copy, scale=e64_sum[:])
             for b in range(n // P):
+                block = slice(b * P, (b + 1) * P)
                 nc.tensor.matmul(
-                    sums_t[u][:, b * P : (b + 1) * P], cp[:, b * P : (b + 1) * P], ident[:],
-                    start=False, stop=(b == n // P - 1), is_transpose=True,
+                    sum_t[u][:, block], scaled[:, block], ident[:], start=False, stop=(b == n // P - 1), is_transpose=True
                 )
-        sts = []
-        dense = []
+        dense_turned = []
         for u, (c0, n) in enumerate(TURNED):
-            sts.append(sb.tile([P, n], F32, name="st%d" % u))
-            nc.scalar.copy(out=sts[u][:], in_=sums_t[u][:, 0:n])
-            dense.append(bank(u, "dense%d" % u))
+            staged = sb.tile([P, n], F32, name="staged%d" % u)
+            nc.scalar.copy(out=staged[:], in_=sum_t[u][:, 0:n])
+            dense_turned.append(bank(u, "dense_turned%d" % u))
             for b in range(n // P):
-                nc.tensor.transpose(dense[u][:, b * P : (b + 1) * P], sts[u][:, b * P : (b + 1) * P], ident[:])
+                block = slice(b * P, (b + 1) * P)
+                nc.tensor.transpose(dense_turned[u][:, block], staged[:, block], ident[:])
 
-        own_cp = sb.tile([P, V - pooled0], F32, name="own_cp")
-        nc.gpsimd.tensor_scalar(own_cp[:], soft[:, pooled0:V], e_sum[:], 0.0, ALU.mult, ALU.add)
-        room = sb.tile([P, 1024], F32, name="room")
-        own = room[:, 256:1024]
-        nc.gpsimd.tensor_tensor(own, own_cp[:], olds[len(TURNED)][:], ALU.add)
+        scaled_pool = sb.tile([P, V - pool0], F32, name="scaled_pool")
+        pool_cols = [slice(c0 - pool0, c0 - pool0 + n) for c0, n in (EARLY, LATE)]
+        for (c0, n), mine in zip((EARLY, LATE), pool_cols):
+            nc.gpsimd.tensor_scalar(scaled_pool[:, mine], soft[:, c0 : c0 + n], e64_sum[:], 0.0, ALU.mult, ALU.add)
+        for mine in pool_cols:
+            nc.gpsimd.tensor_tensor(dense_pool[:, mine], scaled_pool[:, mine], old_pool[:, mine], ALU.add)
 
-        def finish_turned(u, lo, hi):
-            c0 = TURNED[u][0]
-            res = sb.tile([P, hi - lo], F32, name="res%d_%d" % (u, lo))
-            nc.vector.tensor_tensor(res[:], dense[u][:, lo:hi], listed[:, c0 + lo : c0 + hi], ALU.add)
-            nc.sync.dma_start(out=out[:, c0 + lo : c0 + hi], in_=res[:])
+        def finish_on_vector(dense, c0, n):
+            done = sb.tile([P, n], F32, name="done%d" % c0)
+            nc.vector.tensor_tensor(done[:], dense, listed[:, c0 : c0 + n], ALU.add)
+            nc.sync.dma_start(out=out[:, c0 : c0 + n], in_=done[:])
 
-        c0, n = POOLED[0]
-        first = sb.tile([P, n], F32, name="first")
-        nc.vector.tensor_tensor(first[:], own[:, 0:n], listed[:, c0 : c0 + n], ALU.add)
-        nc.sync.dma_start(out=out[:, c0 : c0 + n], in_=first[:])
-        c0, n = POOLED[1]
-        nc.gpsimd.tensor_tensor(room[:, 0:n], own[:, c0 - pooled0 : V - pooled0], listed[:, c0:V], ALU.add)
-        nc.scalar.dma_start(out=out[:, c0:V], in_=room[:, 0:n])
-        finish_turned(0, 0, 256)
-        finish_turned(1, 0, 512)
-        finish_turned(2, 0, 256)
-        finish_turned(2, 256, 512)
+        finish_on_vector(dense_pool[:, pool_cols[0]], *EARLY)
+        nc.gpsimd.tensor_tensor(late_done, dense_pool[:, pool_cols[1]], listed[:, LATE[0] : V], ALU.add)
+        nc.scalar.dma_start(out=out[:, LATE[0] : V], in_=late_done)
+        for u, (c0, n) in enumerate(TURNED):
+            finish_on_vector(dense_turned[u][:, 0:n], c0, n)

from contextlib import ExitStack

import concourse.mybir as mybir
from concourse.masks import make_identity

D, V, Q, I = 512, 2048, 128, 512
FLOPS = 2 * D * V * Q

F32 = mybir.dt.float32
BF16 = mybir.dt.bfloat16
U32 = mybir.dt.uint32
I32 = mybir.dt.int32
U16 = mybir.dt.uint16
U8 = mybir.dt.uint8
FP8X4 = mybir.dt.float8_e4m3fn_x4
ALU = mybir.AluOpType
ACT = mybir.ActivationFunctionType

P = 128
PACK = 4
BANK = 512
GROUPS = V // BANK
HALF = I // 2
QUARTER = I // 4

SHRINK = 2.0**-64

CHUNKS = [(0, 256), (256, 256), (512, 512), (1024, 512), (1536, 512)]

TURNED = [(0, 256), (256, 512), (768, 512)]
EARLY = (1280, 256)
LATE = (1536, 512)


def tile_attend_bdiscouraged_heads_kernel(tc, hid, voc_words, voc_scales, fac, sw, old, offs, out):
    nc = tc.nc
    with ExitStack() as ctx:
        sb = ctx.enter_context(tc.tile_pool(name="sb", bufs=1))
        ps = ctx.enter_context(tc.psum_pool(name="ps", bufs=1))

        def bank(number, name):
            return ps.tile([P, BANK], F32, tag="bank%d" % number, name=name)

        hid_raw = sb.tile([P, PACK, Q], F32, name="hid_raw")
        nc.sync.dma_start(out=hid_raw[:], in_=hid.rearrange("(p t) q -> p t q", t=PACK))

        voc_planes = sb.tile([P, BANK], U8, name="voc_planes", align_bytes=64)
        nc.vector.memset(voc_planes[:].bitcast(I32), 0)

        word_rows = voc_words[0].rearrange("p n t -> p (n t)").bitcast(I32)
        words = [sb.tile([P, BANK], U32, name="words%d" % g, align_bytes=64) for g in range(GROUPS)]

        def load_words(g):
            nc.sync.dma_start(out=words[g][:].bitcast(I32), in_=word_rows[:, g * BANK : (g + 1) * BANK])

        load_words(0)
        scale_rows = voc_scales[0].bitcast(I32)
        for quadrant in range(4):
            nc.sync.dma_start(
                out=voc_planes[32 * quadrant : 32 * quadrant + 4 * GROUPS, :].bitcast(I32),
                in_=scale_rows[4 * quadrant : 4 * quadrant + 4, :].rearrange("r (g c) -> g r c", g=GROUPS),
            )
        for g in range(1, GROUPS):
            load_words(g)
        offsets = sb.tile([P, I // 16], U16, name="offsets")
        nc.sync.dma_start(offsets[:], offs)
        fac_col = sb.tile([P, 1], F32, name="fac_col")
        nc.sync.dma_start(out=fac_col[:], in_=fac)
        sw_rows = sb.tile([P, I], F32, name="sw_rows")
        nc.sync.dma_start(out=sw_rows[:], in_=sw[0].partition_broadcast(P))
        old_turned = []
        for u, (c0, n) in enumerate(TURNED):
            old_turned.append(sb.tile([P, n], F32, name="old_turned%d" % u))
            nc.sync.dma_start(out=old_turned[u][:], in_=old[:, c0 : c0 + n])
        pool0 = EARLY[0]
        old_pool = sb.tile([P, V - pool0], F32, name="old_pool")
        nc.sync.dma_start(out=old_pool[:], in_=old[:, pool0:V])

        listed = sb.tile([P, V], F32, name="listed")
        nc.vector.memset(listed[:], 0.0)
        ident = sb.tile([P, P], F32, name="ident")
        make_identity(nc, ident[:])

        grouped = sb.tile([P, Q, PACK], BF16, name="grouped", align_bytes=64)
        nc.vector.tensor_copy(
            out=grouped[:].rearrange("p (c i) t -> p c t i", i=4),
            in_=hid_raw[:].rearrange("p t (c i) -> p c t i", i=4),
        )
        hid_codes = sb.tile([P, Q], U32, name="hid_codes", align_bytes=64)
        hid_scales = sb.tile([P, Q], U8, name="hid_scales", align_bytes=64)
        nc.vector.quantize_mx(
            out=hid_codes[:].bitcast(FP8X4), scales=hid_scales[:], in_=grouped[:].rearrange("p q t -> p (q t)")
        )

        a = sb.tile([P, V], F32, name="a")
        p_group = sb.tile([P, V], F32, name="p_group")
        chunk_max = sb.tile([P, len(CHUNKS)], F32, name="chunk_max")
        neg_shift = sb.tile([P, GROUPS], F32, name="neg_shift")
        group_sum = sb.tile([P, GROUPS], F32, name="group_sum")
        for j, (c0, n) in enumerate(CHUNKS):
            g, off = divmod(c0, BANK)
            scores = bank(j, "scores%d" % j)
            nc.tensor.matmul_mx(
                out=scores[:, 0:n],
                lhsT=hid_codes[:].bitcast(FP8X4),
                lhsT_scale=hid_scales[:],
                rhs=words[g][:, off : off + n].bitcast(FP8X4),
                rhs_scale=voc_planes[4 * g : P, off : off + n],
                start=True,
                stop=True,
            )
            nc.vector.tensor_scalar(
                a[:, c0 : c0 + n], scores[:, 0:n], 1.0, None, ALU.mult, ALU.max, accum_out=chunk_max[:, j : j + 1]
            )
            if off + n < BANK:
                continue
            since = 0 if g in (0, GROUPS - 1) else j
            nc.vector.tensor_reduce(
                neg_shift[:, g : g + 1], chunk_max[:, since : j + 1], mybir.AxisListType.X, ALU.max, negate=True
            )
            cols = slice(g * BANK, (g + 1) * BANK)
            nc.scalar.activation(
                out=p_group[:, cols],
                in_=a[:, cols],
                func=ACT.Exp,
                bias=neg_shift[:, g : g + 1],
                accum_out=group_sum[:, g : g + 1],
            )
        neg_max = neg_shift[:, GROUPS - 1 : GROUPS]

        picked = sb.tile([P, I], F32, name="picked")
        nc.vector.tensor_copy(picked[:], a[:].indirect(offsets[:]))

        rescale = sb.tile([P, GROUPS], F32, name="rescale")
        nc.scalar.activation(out=rescale[:], in_=neg_shift[:], func=ACT.Exp, scale=-1.0, bias=neg_max)
        halves = [slice(0, HALF), slice(HALF, I)]
        px = sb.tile([P, I], F32, name="px")
        for mine in halves:
            nc.scalar.activation(out=px[:, mine], in_=picked[:, mine], func=ACT.Exp, bias=neg_max)

        neg_terms = sb.tile([P, GROUPS], F32, name="neg_terms")
        neg_z = sb.tile([P, 1], F32, name="neg_z")
        nc.vector.scalar_tensor_tensor(
            neg_terms[:], rescale[:], -1.0, group_sum[:], ALU.mult, ALU.mult, accum_out=neg_z[:]
        )
        neg_z_inv = sb.tile([P, 1], F32, name="neg_z_inv")
        nc.vector.reciprocal(neg_z_inv[:], neg_z[:])
        group_factor = sb.tile([P, GROUPS], F32, name="group_factor")
        nc.scalar.activation(out=group_factor[:], in_=rescale[:], func=ACT.Copy, scale=neg_z_inv[:])
        soft = sb.tile([P, V], F32, name="soft")
        for g in range(GROUPS):
            cols = slice(g * BANK, (g + 1) * BANK)
            nc.scalar.activation(out=soft[:, cols], in_=p_group[:, cols], func=ACT.Copy, scale=group_factor[:, g : g + 1])

        sum_t = []
        for u, (c0, n) in enumerate(TURNED):
            sum_t.append(bank(len(CHUNKS) + u, "sum_t%d" % u))
            for b in range(n // P):
                block = slice(b * P, (b + 1) * P)
                nc.tensor.matmul(
                    sum_t[u][:, block], old_turned[u][:, block], ident[:], start=(b == 0), stop=False, is_transpose=True
                )

        den = sb.tile([P, I], F32, name="den")
        for mine in halves:
            nc.vector.tensor_scalar(den[:, mine], px[:, mine], fac_col[:], neg_z[:], ALU.mult, ALU.subtract)
        pair = sb.tile([P, HALF], F32, name="pair")
        nc.vector.tensor_tensor(pair[:], den[:, 0:HALF], den[:, HALF:I], ALU.mult)
        four = sb.tile([P, QUARTER], F32, name="four")
        nc.vector.scalar_tensor_tensor(four[:], pair[:, 0:QUARTER], SHRINK, pair[:, QUARTER:HALF], ALU.mult, ALU.mult)
        four_inv = sb.tile([P, QUARTER], F32, name="four_inv")
        nc.vector.reciprocal(four_inv[:], four[:])
        pair_inv = sb.tile([P, 2, QUARTER], F32, name="pair_inv")
        nc.vector.scalar_tensor_tensor(
            pair_inv[:],
            pair[:].rearrange("p (s c) -> p s c", s=2)[:, ::-1, :],
            SHRINK,
            four_inv[:].unsqueeze(1).to_broadcast([P, 2, QUARTER]),
            ALU.mult,
            ALU.mult,
        )
        numer = sb.tile([P, I], F32, name="numer")
        crossed = sb.tile([P, I], F32, name="crossed")
        for mine in halves:
            nc.vector.scalar_tensor_tensor(numer[:, mine], px[:, mine], fac_col[:], sw_rows[:, mine], ALU.mult, ALU.mult)
        for mine, partner in zip(halves, reversed(halves)):
            nc.vector.tensor_tensor(crossed[:, mine], numer[:, mine], den[:, partner], ALU.mult)
        e64 = sb.tile([P, I], F32, name="e64")
        e64_sum = sb.tile([P, 1], F32, name="e64_sum")
        nc.vector.scalar_tensor_tensor(
            e64[:].rearrange("p (s c) -> p s c", s=2),
            pair_inv[:].rearrange("p s c -> p (s c)").unsqueeze(1).to_broadcast([P, 2, HALF]),
            -64.0,
            crossed[:].rearrange("p (s c) -> p s c", s=2),
            ALU.mult,
            ALU.mult,
            accum_out=e64_sum[:],
        )
        nc.vector.tensor_copy(listed[:].indirect(offsets[:]), e64[:])

        last = len(TURNED) - 1
        scaled_width = TURNED[last][1]
        shared = sb.tile([P, scaled_width + V - pool0], F32, name="shared")
        dense_pool = shared[:, scaled_width : scaled_width + V - pool0]
        late_done = shared[:, scaled_width + EARLY[1] - LATE[1] : scaled_width + EARLY[1]]

        for u, (c0, n) in enumerate(TURNED):
            scaled = shared[:, 0:n] if u == last else sb.tile([P, n], F32, name="scaled%d" % u)[:]
            nc.scalar.activation(out=scaled, in_=soft[:, c0 : c0 + n], func=ACT.Copy, scale=e64_sum[:])
            for b in range(n // P):
                block = slice(b * P, (b + 1) * P)
                nc.tensor.matmul(
                    sum_t[u][:, block], scaled[:, block], ident[:], start=False, stop=(b == n // P - 1), is_transpose=True
                )
        dense_turned = []
        for u, (c0, n) in enumerate(TURNED):
            staged = sb.tile([P, n], F32, name="staged%d" % u)
            nc.scalar.copy(out=staged[:], in_=sum_t[u][:, 0:n])
            dense_turned.append(bank(u, "dense_turned%d" % u))
            for b in range(n // P):
                block = slice(b * P, (b + 1) * P)
                nc.tensor.transpose(dense_turned[u][:, block], staged[:, block], ident[:])

        scaled_pool = sb.tile([P, V - pool0], F32, name="scaled_pool")
        pool_cols = [slice(c0 - pool0, c0 - pool0 + n) for c0, n in (EARLY, LATE)]
        for (c0, n), mine in zip((EARLY, LATE), pool_cols):
            nc.gpsimd.tensor_scalar(scaled_pool[:, mine], soft[:, c0 : c0 + n], e64_sum[:], 0.0, ALU.mult, ALU.add)
        for mine in pool_cols:
            nc.gpsimd.tensor_tensor(dense_pool[:, mine], scaled_pool[:, mine], old_pool[:, mine], ALU.add)

        def finish_on_vector(dense, c0, n):
            done = sb.tile([P, n], F32, name="done%d" % c0)
            nc.vector.tensor_tensor(done[:], dense, listed[:, c0 : c0 + n], ALU.add)
            nc.sync.dma_start(out=out[:, c0 : c0 + n], in_=done[:])

        finish_on_vector(dense_pool[:, pool_cols[0]], *EARLY)
        nc.gpsimd.tensor_tensor(late_done, dense_pool[:, pool_cols[1]], listed[:, LATE[0] : V], ALU.add)
        nc.scalar.dma_start(out=out[:, LATE[0] : V], in_=late_done)
        for u, (c0, n) in enumerate(TURNED):
            finish_on_vector(dense_turned[u][:, 0:n], c0, n)
